import numpy as np
import ml_dtypes


def mxq(x, axis, fmt="e4m3"):
    dtype, down = {"e4m3": (ml_dtypes.float8_e4m3fn, 7), "e5m2": (ml_dtypes.float8_e5m2, 14)}[fmt]
    v = np.moveaxis(np.asarray(x, np.float32).astype(ml_dtypes.bfloat16).astype(np.float64), axis, -1)
    blocks = v.reshape(v.shape[:-1] + (-1, 32))
    amax = np.abs(blocks).max(-1, keepdims=True)
    byte = np.maximum(np.where(amax > 0, np.frexp(amax)[1] - 1 + 127, 0) - down, 1)
    scale = np.exp2(byte - 127.0)
    codes = (blocks / scale).astype(np.float32).astype(dtype).astype(np.float64)
    return np.moveaxis((codes * scale).reshape(v.shape), -1, axis)


WIDE = False


def mx_kscale(k):
    if not WIDE:
        return np.ones(k)
    levels = np.array([10, -10, 5, -5, 0])
    if k % 512:
        return np.exp2(np.random.permutation(np.resize(levels, k // 32))).repeat(32)
    a = np.empty((k // 512, 16))
    for p in range(k // 512):
        a[p, :8] = np.random.permutation(np.resize(levels, 8))
        for g in range(8):
            far = levels[np.abs(levels - a[p, g]) >= 10]
            a[p, g + 8] = far[np.random.randint(len(far))]
    return np.exp2(a.ravel()).repeat(32)


BF16 = ml_dtypes.bfloat16


def bf(x):
    return np.asarray(x, np.float32).astype(BF16)


def f64(x):
    return np.asarray(x).astype(np.float64)

def planes(Y):
    n, m = Y.shape
    b = f64(bf(Y)).reshape(n // 32, 32, m)
    amax = np.abs(b).max(1)
    byte = np.clip(np.where(amax > 0, np.frexp(amax)[1] - 1 + 127 - 7, 1), 1, 254)
    codes = (b * np.exp2(127.0 - byte)[:, None, :]).reshape(n, m).astype(np.float32).astype(ml_dtypes.float8_e4m3fn).view(np.uint8)
    words = codes.reshape(n // 512, 128, 4, m).transpose(0, 1, 3, 2)
    return np.ascontiguousarray(words), np.ascontiguousarray(byte.astype(np.uint8).reshape(n // 512, 16, m))


B, S, D, F = 3, 1024, 384, 2048


def setup_inputs():
    s = mx_kscale(S)
    spread = np.exp(0.8 * np.random.randn(F))
    x = np.random.randn(B, S, D) * s[None, :, None]
    w_gate = np.random.randn(S, F) / np.sqrt(S) / s[:, None]
    w_up = np.random.randn(S, F) * spread[None, :] / np.sqrt(S) / s[:, None]
    b_gate = 0.5 * np.random.randn(F)
    b_up = 0.4 * np.random.randn(F) * spread
    return {"x": bf(x), "w_gate": bf(w_gate), "b_gate": bf(b_gate), "w_up": bf(w_up), "b_up": bf(b_up)}


def reference(x, w_gate, b_gate, w_up, b_up):
    xq = mxq(f64(x), 1, "e4m3").transpose(1, 0, 2).reshape(S, B * D)
    wg = mxq(f64(w_gate), 0, "e4m3")
    wu = mxq(f64(w_up), 0, "e4m3")
    gate = (wg.T @ xq) + f64(b_gate)[:, None]
    up = (wu.T @ xq) + f64(b_up)[:, None]
    h = gate / (1.0 + np.exp(-gate)) * up
    y = h.reshape(F, B, D).transpose(1, 0, 2)
    Y = y.transpose(1, 0, 2).reshape(F, B * D)
    words, scales = planes(Y)
    return y, words, scales

@@ -1,0 +1,286 @@
+from contextlib import ExitStack
+
+import concourse.mybir as mybir
+
+B, S, D, F = 3, 1024, 384, 2048
+FLOPS = 2 * 2 * F * S * B * D
+
+F32 = mybir.dt.float32
+BF16 = mybir.dt.bfloat16
+I32 = mybir.dt.int32
+U32 = mybir.dt.uint32
+U8 = mybir.dt.uint8
+FP8X4 = mybir.dt.float8_e4m3fn_x4
+SILU = mybir.ActivationFunctionType.Silu
+ADD = mybir.AluOpType.add
+MULT = mybir.AluOpType.mult
+
+P = 128
+PACK = 4
+K_PASS = P * PACK
+PASSES = S // K_PASS
+GROUPS = F // K_PASS
+M = B * D
+STEPS = GROUPS * PACK
+PARTS = 2 * PASSES
+N_SPLIT = ((0, 256), (256, D))
+HALF = 16
+COPY_LEAD = 3
+CAST_START = PACK
+CAST_WIDTH = 256
+
+
+def tile_token_mixing_swiglu_g2_kernel(tc, x, w_gate, b_gate, w_up, b_up, out_0, out_1, out_2):
+    nc = tc.nc
+    weights = (w_gate, w_up)
+
+    with ExitStack() as ctx:
+        keep = ctx.enter_context(tc.tile_pool(name="keep", bufs=1))
+        work = ctx.enter_context(tc.tile_pool(name="work", bufs=1))
+        psum = ctx.enter_context(tc.psum_pool(name="psum", bufs=4))
+        ctx.enter_context(tc.manual_schedule())
+
+        x_raw, x_codes, x_scales, x_side = {}, {}, {}, {}
+        w_raw, w_side, w_codes, w_scales = {}, {}, {}, {}
+        y, y_side, y_codes, silu_of, up_of = {}, {}, {}, {}, {}
+        bias = [keep.tile([P, GROUPS, PACK], BF16, name="bias%d" % i) for i in range(2)]
+        y_scales = keep.tile([P, M], U8, align_bytes=64)
+
+        def copy(on_vector, out, in_):
+            if on_vector:
+                nc.vector.tensor_copy(out=out, in_=in_)
+            else:
+                nc.scalar.copy(out=out, in_=in_)
+
+        def load_x(b, c):
+            x_raw[b, c] = keep.tile([P, PACK, D], BF16, name="x_raw%d_%d" % (b, c))
+            rows = x[b, c * K_PASS : (c + 1) * K_PASS, :]
+            nc.sync.dma_start(out=x_raw[b, c][:], in_=rows.rearrange("(p j) d -> p j d", j=PACK))
+
+        def load_w(g, part):
+            c = part % PASSES
+            w_raw[g, part] = keep.tile([P, PACK, K_PASS], BF16, name="w_raw%d_%d" % (g, part))
+            rows = weights[part // PASSES][c * K_PASS : (c + 1) * K_PASS, g * K_PASS : (g + 1) * K_PASS]
+            nc.sync.dma_start(out=w_raw[g, part][:], in_=rows.rearrange("(p j) f -> p j f", j=PACK))
+
+        def copy_x(b, c):
+            x_side[b, c] = work.tile([P, D, PACK], BF16, name="x_side", tag="x_side", bufs=3, align_bytes=64)
+            dst = x_side[b, c][:].rearrange("p (n i) j -> p n j i", i=4)
+            src = x_raw[b, c][:].rearrange("p j (n i) -> p n j i", i=4)
+            n = D // 8
+            copy(True, dst[:, :n], src[:, :n])
+            copy(False, dst[:, n:], src[:, n:])
+
+        def quantize_x(b, c):
+            x_codes[b, c] = keep.tile([P, D], U32, name="x_codes%d_%d" % (b, c), align_bytes=64)
+            x_scales[b, c] = keep.tile([P, D], U8, name="x_scales%d_%d" % (b, c), align_bytes=64)
+            flat = x_side[b, c][:].rearrange("p d j -> p (d j)")
+            for lo, hi in N_SPLIT:
+                nc.vector.quantize_mx(
+                    out=x_codes[b, c][:, lo:hi].bitcast(FP8X4),
+                    scales=x_scales[b, c][:, lo:hi],
+                    in_=flat[:, PACK * lo : PACK * hi],
+                )
+
+        def copy_w(step, part, lo, hi, on_vector):
+            g, t = divmod(step, PACK)
+            if step not in w_side:
+                w_side[step] = work.tile([P, PARTS, P, PACK], BF16, name="w_side", tag="w_side", bufs=4, align_bytes=64)
+            dst = w_side[step][:, part].rearrange("p (n i) j -> p n j i", i=4)
+            src = w_raw[g, part][:].rearrange("p j (n i t) -> p t n j i", i=4, t=PACK)[:, t]
+            copy(on_vector, dst[:, lo:hi], src[:, lo:hi])
+
+        def copy_w_share(step, first, last, on_vector):
+            for part in range(PARTS):
+                lo, hi = max(first, 2 * part), min(last, 2 * part + 2)
+                if lo < hi:
+                    copy_w(step, part, HALF * (lo - 2 * part), HALF * (hi - 2 * part), on_vector)
+
+        def quantize_w(step):
+            w_codes[step] = work.tile([P, PARTS, P], U32, name="w_codes", tag="w_codes", bufs=3, align_bytes=64)
+            w_scales[step] = work.tile([P, PARTS, P], U8, name="w_scales", tag="w_scales", bufs=3, align_bytes=64)
+            nc.vector.quantize_mx(
+                out=w_codes[step][:].rearrange("p a m -> p (a m)").bitcast(FP8X4),
+                scales=w_scales[step][:].rearrange("p a m -> p (a m)"),
+                in_=w_side[step][:].rearrange("p a m j -> p (a m j)"),
+            )
+
+        def project(step, b, which):
+            bank = psum.tile([P, 512], F32, name="bank%d" % which, tag="bank%d" % which)
+            for lo, hi in N_SPLIT:
+                for c in range(PASSES):
+                    part = which * PASSES + c
+                    nc.tensor.matmul_mx(
+                        out=bank[:, lo:hi],
+                        lhsT=w_codes[step][:, part].bitcast(FP8X4),
+                        lhsT_scale=w_scales[step][:, part],
+                        rhs=x_codes[b, c][:, lo:hi].bitcast(FP8X4),
+                        rhs_scale=x_scales[b, c][:, lo:hi],
+                        start=(c == 0),
+                        stop=(c == PASSES - 1),
+                    )
+            return bank
+
+        def gate_and_up(step, b):
+            g, t = divmod(step, PACK)
+            gate = project(step, b, 0)
+            up_of[step, b] = project(step, b, 1)
+            silu_of[step, b] = work.tile([P, D], F32, name="silu", tag="silu", bufs=4)
+            nc.scalar.activation(out=silu_of[step, b][:], in_=gate[:, :D], func=SILU, bias=bias[0][:, g, t : t + 1])
+
+        def product(step, b):
+            g, t = divmod(step, PACK)
+            if g not in y:
+                y[g] = work.tile([P, PACK, M], F32, name="y", tag="y", bufs=3)
+            nc.vector.scalar_tensor_tensor(
+                out=y[g][:, t, b * D : (b + 1) * D],
+                in0=up_of[step, b][:, :D],
+                scalar=bias[1][:, g, t : t + 1],
+                in1=silu_of[step, b][:],
+                op0=ADD,
+                op1=MULT,
+            )
+
+        def store_y(step, b0, b1):
+            g, t = divmod(step, PACK)
+            rows = out_0[b0:b1, g * K_PASS : (g + 1) * K_PASS, :].rearrange("b (p t) d -> p t b d", t=PACK)
+            nc.sync.dma_start(out=rows[:, t], in_=y[g][:, t, b0 * D : b1 * D].rearrange("p (b d) -> p b d", d=D))
+
+        def cast_y(g, lo, hi, on_vector):
+            if g not in y_side:
+                y_side[g] = work.tile([P, M, PACK], BF16, name="y_side", tag="y_side", bufs=2, align_bytes=64)
+            dst = y_side[g][:, lo:hi].rearrange("p (n i) t -> p n t i", i=4)
+            src = y[g][:, :, lo:hi].rearrange("p t (n i) -> p n t i", i=4)
+            copy(on_vector, dst, src)
+
+        def quantize_y(g, lo, hi):
+            if g not in y_codes:
+                y_codes[g] = work.tile([P, M], U32, name="y_codes", tag="y_codes", bufs=2, align_bytes=64)
+            nc.vector.quantize_mx(
+                out=y_codes[g][:, lo:hi].bitcast(FP8X4),
+                scales=y_scales[PACK * g :, lo:hi],
+                in_=y_side[g][:].rearrange("p m t -> p (m t)")[:, PACK * lo : PACK * hi],
+            )
+
+        def store_codes(g, lo, hi):
+            words = out_1[g].rearrange("p m t -> p (m t)").bitcast(I32)
+            nc.sync.dma_start(out=words[:, lo:hi], in_=y_codes[g][:, lo:hi].bitcast(I32))
+
+        def cast_windows(step):
+            lo = (step - CAST_START) * CAST_WIDTH
+            hi = lo + CAST_WIDTH
+            windows = []
+            for g in range(2):
+                a, z = max(lo, g * M), min(hi, (g + 1) * M)
+                if a < z:
+                    windows.append((g, a - g * M, z - g * M))
+            return windows
+
+        for kind, i, j in (("x", 0, 0), ("x", 0, 1), ("w", 0, 0), ("x", 1, 0), ("w", 0, 1), ("w", 0, 2),
+                           ("x", 1, 1), ("w", 0, 3), ("x", 2, 0), ("x", 2, 1)):
+            if kind == "x":
+                load_x(i, j)
+            else:
+                load_w(i, j)
+        for tile, vec in zip(bias, (b_gate, b_up)):
+            nc.sync.dma_start(out=tile[:], in_=vec.rearrange("(g p t) -> p g t", p=P, t=PACK))
+        for g in range(1, GROUPS):
+            for part in range(PARTS):
+                load_w(g, part)
+
+        warm = keep.tile([P, 8], F32)
+        warmed = keep.tile([P, 8], F32)
+        nc.vector.memset(warm[:], 0.0)
+        nc.scalar.activation(out=warmed[:], in_=warm[:], func=SILU)
+
+        def head_w(part):
+            copy_w(0, part, 0, 2 * HALF, True)
+            copy_w(1, part, 0, 2 * HALF, False)
+            copy_w(2, part, 0, 2 * HALF, True)
+
+        copy_x(0, 0)
+        copy_x(0, 1)
+        quantize_x(0, 0)
+        head_w(0)
+        quantize_x(0, 1)
+        copy_x(1, 0)
+        head_w(1)
+        quantize_x(1, 0)
+        head_w(2)
+        copy_x(1, 1)
+        head_w(3)
+        quantize_x(1, 1)
+        quantize_w(0)
+        copy_x(2, 0)
+        copy_x(2, 1)
+        quantize_x(2, 0)
+        quantize_w(1)
+        quantize_x(2, 1)
+
+        last = STEPS - 1
+        pending = []
+        for step in range(last):
+            ahead = step + COPY_LEAD
+            casts = cast_windows(step)
+            on_scalar = 4 - sum(hi - lo for g, lo, hi in casts) // 128
+            if step > 0:
+                quantize_w(step + 1)
+            gate_and_up(step, 0)
+            product(step, 0)
+            if ahead < STEPS:
+                copy_w_share(ahead, 0, on_scalar, False)
+                copy_w_share(ahead, on_scalar, 6, True)
+            else:
+                lo = (ahead - STEPS) * (M // 2)
+                cast_y(2, lo, lo + 256, False)
+                cast_y(2, lo + 256, lo + M // 2, True)
+            gate_and_up(step, 1)
+            product(step, 1)
+            for g, lo, hi in pending:
+                quantize_y(g, lo, hi)
+                if hi == M:
+                    store_codes(g, 0, M)
+            for g, lo, hi in casts:
+                cast_y(g, lo, hi, False)
+            pending = casts if ahead <= STEPS - 1 else [(2, 0, 512)]
+            if ahead < STEPS:
+                copy_w_share(ahead, 6, 8, True)
+            gate_and_up(step, 2)
+            product(step, 2)
+            store_y(step, 0, B)
+            if step == last - 1:
+                pending = [(2, 512, 1024), (2, 1024, M)]
+
+        g = GROUPS - 1
+        for h, lo, hi in pending:
+            quantize_y(h, lo, hi)
+        store_codes(2, 0, M)
+        gate_and_up(last, 0)
+        product(last, 0)
+        store_y(last, 0, 1)
+        gate_and_up(last, 1)
+        cast_y(g, 0, 256, True)
+        cast_y(g, 256, 384, False)
+        product(last, 1)
+        store_y(last, 1, 2)
+        gate_and_up(last, 2)
+        quantize_y(g, 0, 256)
+        quantize_y(g, 256, 384)
+        store_codes(g, 0, 384)
+        product(last, 2)
+        store_y(last, 2, 3)
+        cast_y(g, 384, 640, False)
+        cast_y(g, 640, 768, True)
+        cast_y(g, 768, 1024, True)
+        cast_y(g, 1024, M, False)
+        quantize_y(g, 384, 640)
+        quantize_y(g, 640, 768)
+        store_codes(g, 384, 768)
+        quantize_y(g, 768, 1024)
+        quantize_y(g, 1024, M)
+        store_codes(g, 768, M)
+        for q in range(4):
+            nc.scalar.dma_start(
+                out=out_2[:, PACK * q : PACK * (q + 1), :].bitcast(I32),
+                in_=y_scales[32 * q : 32 * q + PACK * GROUPS, :].bitcast(I32),
+            )

@@ -24,10 +24,9 @@ M = B * D
 STEPS = GROUPS * PACK
 PARTS = 2 * PASSES
 N_SPLIT = ((0, 256), (256, D))
-HALF = 16
-COPY_LEAD = 3
-CAST_START = PACK
-CAST_WIDTH = 256
+ON_POOL = 192
+S_SHARE = {256: 48, 128: 112}
+COPY_LEAD = 2
 
 
 def tile_token_mixing_swiglu_g2_kernel(tc, x, w_gate, b_gate, w_up, b_up, out_0, out_1, out_2):
@@ -43,11 +42,23 @@ def tile_token_mixing_swiglu_g2_kernel(tc, x, w_gate, b_gate, w_up, b_up, out_0,
         x_raw, x_codes, x_scales, x_side = {}, {}, {}, {}
         w_raw, w_side, w_codes, w_scales = {}, {}, {}, {}
         y, y_side, y_codes, silu_of, up_of = {}, {}, {}, {}, {}
-        bias = [keep.tile([P, GROUPS, PACK], BF16, name="bias%d" % i) for i in range(2)]
+        bias_first = [keep.tile([P, 1, PACK], BF16, name="bias_first%d" % i) for i in range(2)]
+        bias_rest = [keep.tile([P, GROUPS - 1, PACK], BF16, name="bias_rest%d" % i) for i in range(2)]
         y_scales = keep.tile([P, M], U8, align_bytes=64)
 
-        def copy(on_vector, out, in_):
-            if on_vector:
+        def bias(which, step):
+            g, t = divmod(step, PACK)
+            return bias_first[which][:, 0, t : t + 1] if g == 0 else bias_rest[which][:, g - 1, t : t + 1]
+
+        def interleave(engine, dst, src):
+            if engine == "gpsimd":
+                nc.gpsimd.tensor_scalar(
+                    out=dst, in0=src.rearrange("p j m -> p m j"), scalar1=1.0, scalar2=-0.0, op0=MULT, op1=ADD
+                )
+                return
+            out = dst.rearrange("p (n i) j -> p n j i", i=4)
+            in_ = src.rearrange("p j (n i) -> p n j i", i=4)
+            if engine == "vector":
                 nc.vector.tensor_copy(out=out, in_=in_)
             else:
                 nc.scalar.copy(out=out, in_=in_)
@@ -59,22 +70,27 @@ def tile_token_mixing_swiglu_g2_kernel(tc, x, w_gate, b_gate, w_up, b_up, out_0,
 
         def load_w(g, part):
             c = part % PASSES
-            w_raw[g, part] = keep.tile([P, PACK, K_PASS], BF16, name="w_raw%d_%d" % (g, part))
+            if g == 0:
+                w_raw[g, part] = keep.tile([P, PACK, K_PASS], BF16, name="w_first%d" % part)
+                dst = w_raw[g, part][:]
+            else:
+                if g not in w_raw:
+                    w_raw[g] = keep.tile([P, PACK, PARTS, K_PASS], BF16, name="w_raw%d" % g)
+                dst = w_raw[g][:, :, part]
             rows = weights[part // PASSES][c * K_PASS : (c + 1) * K_PASS, g * K_PASS : (g + 1) * K_PASS]
-            nc.sync.dma_start(out=w_raw[g, part][:], in_=rows.rearrange("(p j) f -> p j f", j=PACK))
+            nc.sync.dma_start(out=dst, in_=rows.rearrange("(p j) f -> p j f", j=PACK))
 
-        def copy_x(b, c):
-            x_side[b, c] = work.tile([P, D, PACK], BF16, name="x_side", tag="x_side", bufs=3, align_bytes=64)
-            dst = x_side[b, c][:].rearrange("p (n i) j -> p n j i", i=4)
-            src = x_raw[b, c][:].rearrange("p j (n i) -> p n j i", i=4)
-            n = D // 8
-            copy(True, dst[:, :n], src[:, :n])
-            copy(False, dst[:, n:], src[:, n:])
+        def load_bias(tiles, g0, g1):
+            for tile, vec in zip(tiles, (b_gate, b_up)):
+                nc.sync.dma_start(out=tile[:], in_=vec.rearrange("(g p t) -> p g t", p=P, t=PACK)[:, g0:g1])
+
+        def copy_x(b, c, lo, hi, engine):
+            interleave(engine, x_side[b, c][:, lo:hi], x_raw[b, c][:, :, lo:hi])
 
         def quantize_x(b, c):
             x_codes[b, c] = keep.tile([P, D], U32, name="x_codes%d_%d" % (b, c), align_bytes=64)
             x_scales[b, c] = keep.tile([P, D], U8, name="x_scales%d_%d" % (b, c), align_bytes=64)
-            flat = x_side[b, c][:].rearrange("p d j -> p (d j)")
+            flat = x_side[b, c][:, :D].rearrange("p d j -> p (d j)")
             for lo, hi in N_SPLIT:
                 nc.vector.quantize_mx(
                     out=x_codes[b, c][:, lo:hi].bitcast(FP8X4),
@@ -82,34 +98,34 @@ def tile_token_mixing_swiglu_g2_kernel(tc, x, w_gate, b_gate, w_up, b_up, out_0,
                     in_=flat[:, PACK * lo : PACK * hi],
                 )
 
-        def copy_w(step, part, lo, hi, on_vector):
+        def side_tile(tag):
+            bufs = {"paced": 1, "free": 3}[tag]
+            return work.tile([P, PARTS * P, PACK], BF16, name=tag, tag=tag, bufs=bufs, align_bytes=64)
+
+        def copy_first_w(t, part, engine):
+            src = w_raw[0, part][:].rearrange("p j (m t) -> p t j m", t=PACK)[:, t]
+            interleave(engine, w_side[t][:, part * P : (part + 1) * P], src)
+
+        def copy_w(step, lo, hi, engine):
             g, t = divmod(step, PACK)
-            if step not in w_side:
-                w_side[step] = work.tile([P, PARTS, P, PACK], BF16, name="w_side", tag="w_side", bufs=4, align_bytes=64)
-            dst = w_side[step][:, part].rearrange("p (n i) j -> p n j i", i=4)
-            src = w_raw[g, part][:].rearrange("p j (n i t) -> p t n j i", i=4, t=PACK)[:, t]
-            copy(on_vector, dst[:, lo:hi], src[:, lo:hi])
+            src = w_raw[g][:].rearrange("p j a (m t) -> p t j (a m)", t=PACK)[:, t]
+            interleave(engine, w_side[step][:, lo:hi], src[:, :, lo:hi])
 
-        def copy_w_share(step, first, last, on_vector):
-            for part in range(PARTS):
-                lo, hi = max(first, 2 * part), min(last, 2 * part + 2)
-                if lo < hi:
-                    copy_w(step, part, HALF * (lo - 2 * part), HALF * (hi - 2 * part), on_vector)
-
-        def quantize_w(step):
-            w_codes[step] = work.tile([P, PARTS, P], U32, name="w_codes", tag="w_codes", bufs=3, align_bytes=64)
-            w_scales[step] = work.tile([P, PARTS, P], U8, name="w_scales", tag="w_scales", bufs=3, align_bytes=64)
+        def quantize_w(step, lo, hi):
+            if step not in w_codes:
+                w_codes[step] = work.tile([P, PARTS * P], U32, name="w_codes", tag="w_codes", bufs=6, align_bytes=64)
+                w_scales[step] = work.tile([P, PARTS * P], U8, name="w_scales", tag="w_scales", bufs=6, align_bytes=64)
             nc.vector.quantize_mx(
-                out=w_codes[step][:].rearrange("p a m -> p (a m)").bitcast(FP8X4),
-                scales=w_scales[step][:].rearrange("p a m -> p (a m)"),
-                in_=w_side[step][:].rearrange("p a m j -> p (a m j)"),
+                out=w_codes[step][:, lo:hi].bitcast(FP8X4),
+                scales=w_scales[step][:, lo:hi],
+                in_=w_side[step][:, lo:hi].rearrange("p m j -> p (m j)"),
             )
 
         def project(step, b, which):
             bank = psum.tile([P, 512], F32, name="bank%d" % which, tag="bank%d" % which)
             for lo, hi in N_SPLIT:
                 for c in range(PASSES):
-                    part = which * PASSES + c
+                    part = slice((which * PASSES + c) * P, (which * PASSES + c + 1) * P)
                     nc.tensor.matmul_mx(
                         out=bank[:, lo:hi],
                         lhsT=w_codes[step][:, part].bitcast(FP8X4),
@@ -121,12 +137,17 @@ def tile_token_mixing_swiglu_g2_kernel(tc, x, w_gate, b_gate, w_up, b_up, out_0,
                     )
             return bank
 
-        def gate_and_up(step, b):
-            g, t = divmod(step, PACK)
-            gate = project(step, b, 0)
-            up_of[step, b] = project(step, b, 1)
+        def gate(step, b):
+            bank = project(step, b, 0)
             silu_of[step, b] = work.tile([P, D], F32, name="silu", tag="silu", bufs=4)
-            nc.scalar.activation(out=silu_of[step, b][:], in_=gate[:, :D], func=SILU, bias=bias[0][:, g, t : t + 1])
+            nc.scalar.activation(out=silu_of[step, b][:], in_=bank[:, :D], func=SILU, bias=bias(0, step))
+
+        def up(step, b):
+            up_of[step, b] = project(step, b, 1)
+
+        def gate_and_up(step, b):
+            gate(step, b)
+            up(step, b)
 
         def product(step, b):
             g, t = divmod(step, PACK)
@@ -135,7 +156,7 @@ def tile_token_mixing_swiglu_g2_kernel(tc, x, w_gate, b_gate, w_up, b_up, out_0,
             nc.vector.scalar_tensor_tensor(
                 out=y[g][:, t, b * D : (b + 1) * D],
                 in0=up_of[step, b][:, :D],
-                scalar=bias[1][:, g, t : t + 1],
+                scalar=bias(1, step),
                 in1=silu_of[step, b][:],
                 op0=ADD,
                 op1=MULT,
@@ -146,12 +167,18 @@ def tile_token_mixing_swiglu_g2_kernel(tc, x, w_gate, b_gate, w_up, b_up, out_0,
             rows = out_0[b0:b1, g * K_PASS : (g + 1) * K_PASS, :].rearrange("b (p t) d -> p t b d", t=PACK)
             nc.sync.dma_start(out=rows[:, t], in_=y[g][:, t, b0 * D : b1 * D].rearrange("p (b d) -> p b d", d=D))
 
-        def cast_y(g, lo, hi, on_vector):
-            if g not in y_side:
-                y_side[g] = work.tile([P, M, PACK], BF16, name="y_side", tag="y_side", bufs=2, align_bytes=64)
-            dst = y_side[g][:, lo:hi].rearrange("p (n i) t -> p n t i", i=4)
-            src = y[g][:, :, lo:hi].rearrange("p t (n i) -> p n t i", i=4)
-            copy(on_vector, dst, src)
+        def store_first_y(b):
+            rows = out_0[b, :K_PASS, :].rearrange("(p t) d -> p t d", t=PACK)
+            nc.sync.dma_start(out=rows, in_=y[0][:, :, b * D : (b + 1) * D])
+
+        def open_window(g, lo, hi, wide):
+            if wide:
+                y_side[g, lo] = side_tile("paced")
+            else:
+                y_side[g, lo] = work.tile([P, 256, PACK], BF16, name="y_side", tag="y_side", bufs=5, align_bytes=64)
+
+        def cast_y(g, start, lo, hi, engine):
+            interleave(engine, y_side[g, start][:, lo - start : hi - start], y[g][:, :, lo:hi])
 
         def quantize_y(g, lo, hi):
             if g not in y_codes:
@@ -159,108 +186,129 @@ def tile_token_mixing_swiglu_g2_kernel(tc, x, w_gate, b_gate, w_up, b_up, out_0,
             nc.vector.quantize_mx(
                 out=y_codes[g][:, lo:hi].bitcast(FP8X4),
                 scales=y_scales[PACK * g :, lo:hi],
-                in_=y_side[g][:].rearrange("p m t -> p (m t)")[:, PACK * lo : PACK * hi],
+                in_=y_side[g, lo][:, : hi - lo].rearrange("p m t -> p (m t)"),
             )
 
         def store_codes(g, lo, hi):
             words = out_1[g].rearrange("p m t -> p (m t)").bitcast(I32)
             nc.sync.dma_start(out=words[:, lo:hi], in_=y_codes[g][:, lo:hi].bitcast(I32))
 
-        def cast_windows(step):
-            lo = (step - CAST_START) * CAST_WIDTH
-            hi = lo + CAST_WIDTH
-            windows = []
-            for g in range(2):
-                a, z = max(lo, g * M), min(hi, (g + 1) * M)
-                if a < z:
-                    windows.append((g, a - g * M, z - g * M))
-            return windows
-
-        for kind, i, j in (("x", 0, 0), ("x", 0, 1), ("w", 0, 0), ("x", 1, 0), ("w", 0, 1), ("w", 0, 2),
-                           ("x", 1, 1), ("w", 0, 3), ("x", 2, 0), ("x", 2, 1)):
+        for kind, i, j in (("x", 0, 0), ("w", 0, 0), ("x", 0, 1), ("w", 0, 1), ("w", 0, 2), ("w", 0, 3)):
             if kind == "x":
                 load_x(i, j)
             else:
                 load_w(i, j)
-        for tile, vec in zip(bias, (b_gate, b_up)):
-            nc.sync.dma_start(out=tile[:], in_=vec.rearrange("(g p t) -> p g t", p=P, t=PACK))
+        load_bias(bias_first, 0, 1)
+        for b in range(1, B):
+            for c in range(PASSES):
+                load_x(b, c)
         for g in range(1, GROUPS):
             for part in range(PARTS):
                 load_w(g, part)
+            if g == 1:
+                load_bias(bias_rest, 1, GROUPS)
 
         warm = keep.tile([P, 8], F32)
         warmed = keep.tile([P, 8], F32)
         nc.vector.memset(warm[:], 0.0)
         nc.scalar.activation(out=warmed[:], in_=warm[:], func=SILU)
 
-        def head_w(part):
-            copy_w(0, part, 0, 2 * HALF, True)
-            copy_w(1, part, 0, 2 * HALF, False)
-            copy_w(2, part, 0, 2 * HALF, True)
+        def x_tile():
+            return work.tile([P, D, PACK], BF16, name="x_side", tag="x_side", bufs=2, align_bytes=64)
 
-        copy_x(0, 0)
-        copy_x(0, 1)
-        quantize_x(0, 0)
-        head_w(0)
-        quantize_x(0, 1)
-        copy_x(1, 0)
-        head_w(1)
-        quantize_x(1, 0)
-        head_w(2)
-        copy_x(1, 1)
-        head_w(3)
-        quantize_x(1, 1)
-        quantize_w(0)
-        copy_x(2, 0)
-        copy_x(2, 1)
-        quantize_x(2, 0)
-        quantize_w(1)
-        quantize_x(2, 1)
+        def head_x(c):
+            x_side[0, c] = x_tile()
+            copy_x(0, c, 0, D // 2, "vector")
+            copy_x(0, c, D // 2, D, "scalar")
+            quantize_x(0, c)
 
+        def head_w(part, on_vector):
+            for t in range(PACK):
+                copy_first_w(t, part, "vector" if t < on_vector else "scalar")
+
+        for t in range(PACK):
+            w_side[t] = side_tile("paced" if t == PACK - 1 else "free")
+        head_x(0)
+        head_w(0, 3)
+        head_x(1)
+        head_w(1, 2)
+        quantize_w(0, 0, 256)
+        quantize_w(1, 0, 256)
+        head_w(2, 2)
+        quantize_w(2, 0, 256)
+        quantize_w(3, 0, 256)
+        head_w(3, 2)
+        for t in range(PACK):
+            gate(t, 0)
+        for t in range(PACK):
+            quantize_w(t, 256, 512)
+            up(t, 0)
+
+        units = [(t, b) for b in range(B) for t in range(PACK)]
+        units += [(step, b) for step in range(PACK, STEPS) for b in range(B)]
+        casts_of = {
+            2: [(0, 0, 256)], 3: [(0, 256, 384)], 4: [(0, 384, 640)], 5: [(0, 640, 768)], 6: [(0, 768, 1024)],
+            7: [(0, 1024, M)], 8: [(1, 0, 256)], 9: [(1, 256, 512)], 10: [(1, 512, 768)], 11: [(1, 768, 1024)],
+            12: [(1, 1024, M), (2, 0, 128)], 13: [(2, 128, 384)], 14: [(2, 384, 640)],
+        }
         last = STEPS - 1
         pending = []
-        for step in range(last):
-            ahead = step + COPY_LEAD
-            casts = cast_windows(step)
-            on_scalar = 4 - sum(hi - lo for g, lo, hi in casts) // 128
-            if step > 0:
-                quantize_w(step + 1)
-            gate_and_up(step, 0)
-            product(step, 0)
-            if ahead < STEPS:
-                copy_w_share(ahead, 0, on_scalar, False)
-                copy_w_share(ahead, on_scalar, 6, True)
+        for slot in range(last):
+            ahead = slot + COPY_LEAD
+            casts = casts_of.get(slot, [])
+            if slot in (1, 2):
+                quantize_x(slot, 0)
+            elif slot > 2:
+                quantize_w(slot + 1, 0, PARTS * P)
+            for step, b in units[B * slot : B * (slot + 1)]:
+                if step >= PACK or b > 0:
+                    gate_and_up(step, b)
+                product(step, b)
+                if step == PACK - 1:
+                    store_first_y(b)
+            if slot >= PACK:
+                store_y(slot, 0, B)
+            if slot < 2:
+                b = slot + 1
+                x_side[b, 0] = side_tile("paced")
+                x_side[b, 1] = x_tile()
+                copy_x(b, 0, 0, ON_POOL, "gpsimd")
+                copy_x(b, 1, 272, D, "scalar")
+                copy_x(b, 0, ON_POOL, D, "scalar")
+                copy_x(b, 1, 0, 272, "vector")
+                quantize_x(b, 1)
+            elif ahead < STEPS:
+                on_scalar = S_SHARE[sum(hi - lo for g, lo, hi in casts)]
+                w_side[ahead] = side_tile("paced")
+                copy_w(ahead, 0, ON_POOL, "gpsimd")
+                copy_w(ahead, ON_POOL, ON_POOL + on_scalar, "scalar")
+                copy_w(ahead, ON_POOL + on_scalar, PARTS * P, "vector")
             else:
-                lo = (ahead - STEPS) * (M // 2)
-                cast_y(2, lo, lo + 256, False)
-                cast_y(2, lo + 256, lo + M // 2, True)
-            gate_and_up(step, 1)
-            product(step, 1)
+                open_window(2, 640, M, True)
+                cast_y(2, 640, 640, 640 + ON_POOL, "gpsimd")
+                cast_y(2, 640, 640 + ON_POOL, 880, "scalar")
+                cast_y(2, 640, 880, M, "vector")
             for g, lo, hi in pending:
                 quantize_y(g, lo, hi)
                 if hi == M:
                     store_codes(g, 0, M)
             for g, lo, hi in casts:
-                cast_y(g, lo, hi, False)
-            pending = casts if ahead <= STEPS - 1 else [(2, 0, 512)]
-            if ahead < STEPS:
-                copy_w_share(ahead, 6, 8, True)
-            gate_and_up(step, 2)
-            product(step, 2)
-            store_y(step, 0, B)
-            if step == last - 1:
-                pending = [(2, 512, 1024), (2, 1024, M)]
+                open_window(g, lo, hi, False)
+                cast_y(g, lo, lo, hi, "scalar")
+            pending = casts
 
         g = GROUPS - 1
-        for h, lo, hi in pending:
-            quantize_y(h, lo, hi)
-        store_codes(2, 0, M)
+        quantize_y(2, 384, 640)
         gate_and_up(last, 0)
         product(last, 0)
         store_y(last, 0, 1)
+        quantize_y(2, 640, M)
+        store_codes(2, 0, M)
         gate_and_up(last, 1)
-        cast_y(g, 0, 256, True)
-        cast_y(g, 256, 384, False)
+        open_window(g, 0, 256, False)
+        cast_y(g, 0, 0, 256, "vector")
+        open_window(g, 256, 384, False)
+        cast_y(g, 256, 256, 384, "scalar")
         product(last, 1)
         store_y(last, 1, 2)
         gate_and_up(last, 2)
@@ -269,12 +317,16 @@ def tile_token_mixing_swiglu_g2_kernel(tc, x, w_gate, b_gate, w_up, b_up, out_0,
         store_codes(g, 0, 384)
         product(last, 2)
         store_y(last, 2, 3)
-        cast_y(g, 384, 640, False)
-        cast_y(g, 640, 768, True)
-        cast_y(g, 768, 1024, True)
-        cast_y(g, 1024, M, False)
-        quantize_y(g, 384, 640)
+        open_window(g, 384, 640, False)
+        cast_y(g, 384, 384, 640, "scalar")
+        open_window(g, 640, 768, False)
+        cast_y(g, 640, 640, 768, "vector")
+        open_window(g, 768, 1024, False)
+        cast_y(g, 768, 768, 1024, "vector")
+        open_window(g, 1024, M, False)
+        cast_y(g, 1024, 1024, M, "scalar")
         quantize_y(g, 640, 768)
+        quantize_y(g, 384, 640)
         store_codes(g, 384, 768)
         quantize_y(g, 768, 1024)
         quantize_y(g, 1024, M)

@@ -24,8 +24,13 @@ M = B * D
 STEPS = GROUPS * PACK
 PARTS = 2 * PASSES
 N_SPLIT = ((0, 256), (256, D))
-ON_POOL = 192
-S_SHARE = {256: 48, 128: 112}
+X_POOL = (64, 160)
+X_VECTOR = (288, 256)
+S_COLUMNS = (304, 328)
+ON_POOL = 128
+EXTRA = 96
+HEAD_W = (3, 2, 3, 2)
+HEAD_X = (256, 256)
 COPY_LEAD = 2
 
 
@@ -50,14 +55,14 @@ def tile_token_mixing_swiglu_g2_kernel(tc, x, w_gate, b_gate, w_up, b_up, out_0,
             g, t = divmod(step, PACK)
             return bias_first[which][:, 0, t : t + 1] if g == 0 else bias_rest[which][:, g - 1, t : t + 1]
 
-        def interleave(engine, dst, src):
+        def interleave(engine, dst, src, run=4):
             if engine == "gpsimd":
                 nc.gpsimd.tensor_scalar(
                     out=dst, in0=src.rearrange("p j m -> p m j"), scalar1=1.0, scalar2=-0.0, op0=MULT, op1=ADD
                 )
                 return
-            out = dst.rearrange("p (n i) j -> p n j i", i=4)
-            in_ = src.rearrange("p j (n i) -> p n j i", i=4)
+            out = dst.rearrange("p (n i) j -> p n j i", i=run)
+            in_ = src.rearrange("p j (n i) -> p n j i", i=run)
             if engine == "vector":
                 nc.vector.tensor_copy(out=out, in_=in_)
             else:
@@ -87,11 +92,12 @@ def tile_token_mixing_swiglu_g2_kernel(tc, x, w_gate, b_gate, w_up, b_up, out_0,
         def copy_x(b, c, lo, hi, engine):
             interleave(engine, x_side[b, c][:, lo:hi], x_raw[b, c][:, :, lo:hi])
 
-        def quantize_x(b, c):
-            x_codes[b, c] = keep.tile([P, D], U32, name="x_codes%d_%d" % (b, c), align_bytes=64)
-            x_scales[b, c] = keep.tile([P, D], U8, name="x_scales%d_%d" % (b, c), align_bytes=64)
+        def quantize_x(b, c, windows):
+            if (b, c) not in x_codes:
+                x_codes[b, c] = keep.tile([P, D], U32, name="x_codes%d_%d" % (b, c), align_bytes=64)
+                x_scales[b, c] = keep.tile([P, D], U8, name="x_scales%d_%d" % (b, c), align_bytes=64)
             flat = x_side[b, c][:, :D].rearrange("p d j -> p (d j)")
-            for lo, hi in N_SPLIT:
+            for lo, hi in windows:
                 nc.vector.quantize_mx(
                     out=x_codes[b, c][:, lo:hi].bitcast(FP8X4),
                     scales=x_scales[b, c][:, lo:hi],
@@ -104,12 +110,12 @@ def tile_token_mixing_swiglu_g2_kernel(tc, x, w_gate, b_gate, w_up, b_up, out_0,
 
         def copy_first_w(t, part, engine):
             src = w_raw[0, part][:].rearrange("p j (m t) -> p t j m", t=PACK)[:, t]
-            interleave(engine, w_side[t][:, part * P : (part + 1) * P], src)
+            interleave(engine, w_side[t][:, part * P : (part + 1) * P], src, 2)
 
         def copy_w(step, lo, hi, engine):
             g, t = divmod(step, PACK)
             src = w_raw[g][:].rearrange("p j a (m t) -> p t j (a m)", t=PACK)[:, t]
-            interleave(engine, w_side[step][:, lo:hi], src[:, :, lo:hi])
+            interleave(engine, w_side[step][:, lo:hi], src[:, :, lo:hi], 2)
 
         def quantize_w(step, lo, hi):
             if step not in w_codes:
@@ -175,18 +181,19 @@ def tile_token_mixing_swiglu_g2_kernel(tc, x, w_gate, b_gate, w_up, b_up, out_0,
             if wide:
                 y_side[g, lo] = side_tile("paced")
             else:
-                y_side[g, lo] = work.tile([P, 256, PACK], BF16, name="y_side", tag="y_side", bufs=5, align_bytes=64)
+                y_side[g, lo] = work.tile([P, 256, PACK], BF16, name="y_side", tag="y_side", bufs=6, align_bytes=64)
 
         def cast_y(g, start, lo, hi, engine):
             interleave(engine, y_side[g, start][:, lo - start : hi - start], y[g][:, :, lo:hi])
 
-        def quantize_y(g, lo, hi):
+        def quantize_y(g, lo, hi, start=None):
+            start = lo if start is None else start
             if g not in y_codes:
                 y_codes[g] = work.tile([P, M], U32, name="y_codes", tag="y_codes", bufs=2, align_bytes=64)
             nc.vector.quantize_mx(
                 out=y_codes[g][:, lo:hi].bitcast(FP8X4),
                 scales=y_scales[PACK * g :, lo:hi],
-                in_=y_side[g, lo][:, : hi - lo].rearrange("p m t -> p (m t)"),
+                in_=y_side[g, start][:, lo - start : hi - start].rearrange("p m t -> p (m t)"),
             )
 
         def store_codes(g, lo, hi):
@@ -218,9 +225,9 @@ def tile_token_mixing_swiglu_g2_kernel(tc, x, w_gate, b_gate, w_up, b_up, out_0,
 
         def head_x(c):
             x_side[0, c] = x_tile()
-            copy_x(0, c, 0, D // 2, "vector")
-            copy_x(0, c, D // 2, D, "scalar")
-            quantize_x(0, c)
+            copy_x(0, c, 0, HEAD_X[c], "vector")
+            copy_x(0, c, HEAD_X[c], D, "scalar")
+            quantize_x(0, c, N_SPLIT[::-1])
 
         def head_w(part, on_vector):
             for t in range(PACK):
@@ -229,102 +236,104 @@ def tile_token_mixing_swiglu_g2_kernel(tc, x, w_gate, b_gate, w_up, b_up, out_0,
         for t in range(PACK):
             w_side[t] = side_tile("paced" if t == PACK - 1 else "free")
         head_x(0)
-        head_w(0, 3)
+        head_w(0, HEAD_W[0])
         head_x(1)
-        head_w(1, 2)
+        head_w(1, HEAD_W[1])
         quantize_w(0, 0, 256)
         quantize_w(1, 0, 256)
-        head_w(2, 2)
+        head_w(2, HEAD_W[2])
         quantize_w(2, 0, 256)
         quantize_w(3, 0, 256)
-        head_w(3, 2)
+        head_w(3, HEAD_W[3])
         for t in range(PACK):
             gate(t, 0)
         for t in range(PACK):
             quantize_w(t, 256, 512)
+        for t in range(PACK):
             up(t, 0)
 
         units = [(t, b) for b in range(B) for t in range(PACK)]
-        units += [(step, b) for step in range(PACK, STEPS) for b in range(B)]
-        casts_of = {
-            2: [(0, 0, 256)], 3: [(0, 256, 384)], 4: [(0, 384, 640)], 5: [(0, 640, 768)], 6: [(0, 768, 1024)],
-            7: [(0, 1024, M)], 8: [(1, 0, 256)], 9: [(1, 256, 512)], 10: [(1, 512, 768)], 11: [(1, 768, 1024)],
-            12: [(1, 1024, M), (2, 0, 128)], 13: [(2, 128, 384)], 14: [(2, 384, 640)],
-        }
+        units += [(step, b) for step in range(PACK, STEPS - 2) for b in range(B)]
+        units += [(STEPS - 2, 0), (STEPS - 2, 1), (STEPS - 1, 0), (STEPS - 1, 1), (STEPS - 2, 2), (STEPS - 1, 2)]
+        sizes = [2, 3, 4] + [B] * (STEPS - 3)
+        paced = {slot: (0, 192 * (slot - 2), 192 * (slot - 1)) for slot in range(2, 8)}
+        paced.update({slot: (1, 256 * (slot - 8), 256 * (slot - 7)) for slot in range(8, 12)})
+        paced.update({slot: (2, 256 * (slot - 12), 256 * (slot - 11)) for slot in range(12, 15)})
         last = STEPS - 1
-        pending = []
         for slot in range(last):
             ahead = slot + COPY_LEAD
-            casts = casts_of.get(slot, [])
-            if slot in (1, 2):
-                quantize_x(slot, 0)
-            elif slot > 2:
-                quantize_w(slot + 1, 0, PARTS * P)
-            for step, b in units[B * slot : B * (slot + 1)]:
+            for step, b in units[sum(sizes[:slot]) : sum(sizes[: slot + 1])]:
                 if step >= PACK or b > 0:
                     gate_and_up(step, b)
                 product(step, b)
                 if step == PACK - 1:
                     store_first_y(b)
-            if slot >= PACK:
+                if step >= STEPS - 2:
+                    store_y(step, b, b + 1)
+            if PACK <= slot < STEPS - 2:
                 store_y(slot, 0, B)
             if slot < 2:
                 b = slot + 1
+                on_pool = X_POOL[slot]
                 x_side[b, 0] = side_tile("paced")
                 x_side[b, 1] = x_tile()
-                copy_x(b, 0, 0, ON_POOL, "gpsimd")
-                copy_x(b, 1, 272, D, "scalar")
-                copy_x(b, 0, ON_POOL, D, "scalar")
-                copy_x(b, 1, 0, 272, "vector")
-                quantize_x(b, 1)
-            elif ahead < STEPS:
-                on_scalar = S_SHARE[sum(hi - lo for g, lo, hi in casts)]
-                w_side[ahead] = side_tile("paced")
-                copy_w(ahead, 0, ON_POOL, "gpsimd")
-                copy_w(ahead, ON_POOL, ON_POOL + on_scalar, "scalar")
-                copy_w(ahead, ON_POOL + on_scalar, PARTS * P, "vector")
+                copy_x(b, 0, 0, on_pool, "gpsimd")
+                copy_x(b, 0, on_pool, D, "scalar")
+                copy_x(b, 1, X_VECTOR[slot], D, "scalar")
+                copy_x(b, 1, 0, X_VECTOR[slot], "vector")
+                quantize_x(b, 0, N_SPLIT[1:])
+                quantize_x(b, 1, N_SPLIT)
+                quantize_x(b, 0, N_SPLIT[:1])
+                continue
+            g, lo, hi = paced[slot]
+            open_window(g, lo, hi, True)
+            cast_y(g, lo, lo, lo + ON_POOL, "gpsimd")
+            cast_y(g, lo, lo + ON_POOL, hi, "scalar")
+            extra = {12: 1, 14: 2}.get(slot)
+            if extra:
+                open_window(extra, 1024, M, False)
+                cast_y(extra, 1024, 1024, M, "scalar")
+            if ahead < STEPS:
+                on_scalar = S_COLUMNS[slot >= 8] - (hi - lo - ON_POOL) - (EXTRA if extra else 0)
+                w_side[ahead] = side_tile("free")
+                copy_w(ahead, 0, on_scalar, "scalar")
+                if on_scalar < 256:
+                    copy_w(ahead, on_scalar, 256, "vector")
+                copy_w(ahead, 256, PARTS * P, "vector")
+                quantize_w(ahead, 0, 256)
+                if extra:
+                    quantize_y(extra, 1024, M)
+                    store_codes(extra, 0, M)
+                if hi - lo == 192:
+                    quantize_y(g, lo + 128, hi, lo)
+                    quantize_y(g, lo, lo + 128)
+                else:
+                    quantize_y(g, lo, hi)
+                quantize_w(ahead, 256, PARTS * P)
             else:
-                open_window(2, 640, M, True)
-                cast_y(2, 640, 640, 640 + ON_POOL, "gpsimd")
-                cast_y(2, 640, 640 + ON_POOL, 880, "scalar")
-                cast_y(2, 640, 880, M, "vector")
-            for g, lo, hi in pending:
+                open_window(2, 768, 1024, False)
+                cast_y(2, 768, 768, 1024, "vector")
                 quantize_y(g, lo, hi)
-                if hi == M:
-                    store_codes(g, 0, M)
-            for g, lo, hi in casts:
-                open_window(g, lo, hi, False)
-                cast_y(g, lo, lo, hi, "scalar")
-            pending = casts
+                quantize_y(2, 768, 1024)
+            if (g, hi) == (0, M):
+                store_codes(0, 0, M)
 
         g = GROUPS - 1
-        quantize_y(2, 384, 640)
-        gate_and_up(last, 0)
-        product(last, 0)
-        store_y(last, 0, 1)
-        quantize_y(2, 640, M)
+        for step, b in units[-B:]:
+            gate_and_up(step, b)
+            product(step, b)
+            store_y(step, b, b + 1)
+        for lo, hi, engine in ((0, 128, "gpsimd"), (128, 384, "scalar"), (384, 640, "scalar"), (640, 768, "vector")):
+            open_window(g, lo, hi, engine == "gpsimd")
+            cast_y(g, lo, lo, hi, engine)
+        quantize_y(2, 1024, M)
         store_codes(2, 0, M)
-        gate_and_up(last, 1)
-        open_window(g, 0, 256, False)
-        cast_y(g, 0, 0, 256, "vector")
-        open_window(g, 256, 384, False)
-        cast_y(g, 256, 256, 384, "scalar")
-        product(last, 1)
-        store_y(last, 1, 2)
-        gate_and_up(last, 2)
-        quantize_y(g, 0, 256)
-        quantize_y(g, 256, 384)
+        quantize_y(g, 0, 128)
+        quantize_y(g, 128, 384)
         store_codes(g, 0, 384)
-        product(last, 2)
-        store_y(last, 2, 3)
-        open_window(g, 384, 640, False)
-        cast_y(g, 384, 384, 640, "scalar")
-        open_window(g, 640, 768, False)
-        cast_y(g, 640, 640, 768, "vector")
-        open_window(g, 768, 1024, False)
-        cast_y(g, 768, 768, 1024, "vector")
-        open_window(g, 1024, M, False)
-        cast_y(g, 1024, 1024, M, "scalar")
+        for lo, hi, engine in ((768, 1024, "vector"), (1024, M, "scalar")):
+            open_window(g, lo, hi, False)
+            cast_y(g, lo, lo, hi, engine)
         quantize_y(g, 640, 768)
         quantize_y(g, 384, 640)
         store_codes(g, 384, 768)
@@ -332,7 +341,7 @@ def tile_token_mixing_swiglu_g2_kernel(tc, x, w_gate, b_gate, w_up, b_up, out_0,
         quantize_y(g, 1024, M)
         store_codes(g, 768, M)
         for q in range(4):
-            nc.scalar.dma_start(
+            (nc.scalar if q % 2 else nc.sync).dma_start(
                 out=out_2[:, PACK * q : PACK * (q + 1), :].bitcast(I32),
                 in_=y_scales[32 * q : 32 * q + PACK * GROUPS, :].bitcast(I32),
             )

@@ -23,15 +23,20 @@ GROUPS = F // K_PASS
 M = B * D
 STEPS = GROUPS * PACK
 PARTS = 2 * PASSES
+W_COLUMNS = PARTS * P
+X_COLUMNS = PASSES * D
 N_SPLIT = ((0, 256), (256, D))
-X_POOL = (64, 160)
-X_VECTOR = (288, 256)
-S_COLUMNS = (304, 328)
-ON_POOL = 128
-EXTRA = 96
+WIDE = 512
+PACED = 256
 HEAD_W = (3, 2, 3, 2)
 HEAD_X = (256, 256)
-COPY_LEAD = 2
+X_VECTOR = 224
+W_SCALAR = 192
+W_SCALAR_EARLY = (256, 320)
+W_CUT = 336
+Y_SCALAR = (256, 256)
+W_RUN = 4
+Y_PITCH = PACK * D + PACED
 
 
 def tile_token_mixing_swiglu_g2_kernel(tc, x, w_gate, b_gate, w_up, b_up, out_0, out_1, out_2):
@@ -44,12 +49,12 @@ def tile_token_mixing_swiglu_g2_kernel(tc, x, w_gate, b_gate, w_up, b_up, out_0,
         psum = ctx.enter_context(tc.psum_pool(name="psum", bufs=4))
         ctx.enter_context(tc.manual_schedule())
 
-        x_raw, x_codes, x_scales, x_side = {}, {}, {}, {}
+        x_raw, x_codes, x_scales = {}, {}, {}
         w_raw, w_side, w_codes, w_scales = {}, {}, {}, {}
         y, y_side, y_codes, silu_of, up_of = {}, {}, {}, {}, {}
         bias_first = [keep.tile([P, 1, PACK], BF16, name="bias_first%d" % i) for i in range(2)]
         bias_rest = [keep.tile([P, GROUPS - 1, PACK], BF16, name="bias_rest%d" % i) for i in range(2)]
-        y_scales = keep.tile([P, M], U8, align_bytes=64)
+        y_scales = keep.tile([P, M], U8, name="y_scales", align_bytes=64)
 
         def bias(which, step):
             g, t = divmod(step, PACK)
@@ -67,6 +72,15 @@ def tile_token_mixing_swiglu_g2_kernel(tc, x, w_gate, b_gate, w_up, b_up, out_0,
                 nc.vector.tensor_copy(out=out, in_=in_)
             else:
                 nc.scalar.copy(out=out, in_=in_)
+
+        def quantize(codes, scales, side):
+            nc.vector.quantize_mx(out=codes.bitcast(FP8X4), scales=scales, in_=side.rearrange("p m j -> p (m j)"))
+
+        def wide_tile():
+            return work.tile([P, WIDE, PACK], BF16, name="wide", tag="wide", bufs=6, align_bytes=64)
+
+        def paced_tile():
+            return work.tile([P, PACED, PACK], BF16, name="paced", tag="paced", bufs=1, align_bytes=64)
 
         def load_x(b, c):
             x_raw[b, c] = keep.tile([P, PACK, D], BF16, name="x_raw%d_%d" % (b, c))
@@ -89,55 +103,41 @@ def tile_token_mixing_swiglu_g2_kernel(tc, x, w_gate, b_gate, w_up, b_up, out_0,
             for tile, vec in zip(tiles, (b_gate, b_up)):
                 nc.sync.dma_start(out=tile[:], in_=vec.rearrange("(g p t) -> p g t", p=P, t=PACK)[:, g0:g1])
 
-        def copy_x(b, c, lo, hi, engine):
-            interleave(engine, x_side[b, c][:, lo:hi], x_raw[b, c][:, :, lo:hi])
-
-        def quantize_x(b, c, windows):
-            if (b, c) not in x_codes:
-                x_codes[b, c] = keep.tile([P, D], U32, name="x_codes%d_%d" % (b, c), align_bytes=64)
-                x_scales[b, c] = keep.tile([P, D], U8, name="x_scales%d_%d" % (b, c), align_bytes=64)
-            flat = x_side[b, c][:, :D].rearrange("p d j -> p (d j)")
-            for lo, hi in windows:
-                nc.vector.quantize_mx(
-                    out=x_codes[b, c][:, lo:hi].bitcast(FP8X4),
-                    scales=x_scales[b, c][:, lo:hi],
-                    in_=flat[:, PACK * lo : PACK * hi],
-                )
-
-        def side_tile(tag):
-            bufs = {"paced": 1, "free": 3}[tag]
-            return work.tile([P, PARTS * P, PACK], BF16, name=tag, tag=tag, bufs=bufs, align_bytes=64)
+        def quantize_x(b, lo, hi, side):
+            if b not in x_codes:
+                x_codes[b] = keep.tile([P, X_COLUMNS], U32, name="x_codes%d" % b, align_bytes=64)
+                x_scales[b] = keep.tile([P, X_COLUMNS], U8, name="x_scales%d" % b, align_bytes=64)
+            quantize(x_codes[b][:, lo:hi], x_scales[b][:, lo:hi], side)
 
         def copy_first_w(t, part, engine):
             src = w_raw[0, part][:].rearrange("p j (m t) -> p t j m", t=PACK)[:, t]
-            interleave(engine, w_side[t][:, part * P : (part + 1) * P], src, 2)
+            interleave(engine, w_side[t][:, part * P : (part + 1) * P], src, W_RUN)
 
         def copy_w(step, lo, hi, engine):
             g, t = divmod(step, PACK)
+            if step not in w_side:
+                w_side[step] = wide_tile()
             src = w_raw[g][:].rearrange("p j a (m t) -> p t j (a m)", t=PACK)[:, t]
-            interleave(engine, w_side[step][:, lo:hi], src[:, :, lo:hi], 2)
+            interleave(engine, w_side[step][:, lo:hi], src[:, :, lo:hi], W_RUN)
 
-        def quantize_w(step, lo, hi):
+        def quantize_w(step, lo=0, hi=W_COLUMNS):
             if step not in w_codes:
-                w_codes[step] = work.tile([P, PARTS * P], U32, name="w_codes", tag="w_codes", bufs=6, align_bytes=64)
-                w_scales[step] = work.tile([P, PARTS * P], U8, name="w_scales", tag="w_scales", bufs=6, align_bytes=64)
-            nc.vector.quantize_mx(
-                out=w_codes[step][:, lo:hi].bitcast(FP8X4),
-                scales=w_scales[step][:, lo:hi],
-                in_=w_side[step][:, lo:hi].rearrange("p m j -> p (m j)"),
-            )
+                w_codes[step] = work.tile([P, W_COLUMNS], U32, name="w_codes", tag="w_codes", bufs=7, align_bytes=64)
+                w_scales[step] = work.tile([P, W_COLUMNS], U8, name="w_scales", tag="w_scales", bufs=7, align_bytes=64)
+            quantize(w_codes[step][:, lo:hi], w_scales[step][:, lo:hi], w_side[step][:, lo:hi])
 
         def project(step, b, which):
             bank = psum.tile([P, 512], F32, name="bank%d" % which, tag="bank%d" % which)
             for lo, hi in N_SPLIT:
                 for c in range(PASSES):
                     part = slice((which * PASSES + c) * P, (which * PASSES + c + 1) * P)
+                    columns = slice(c * D + lo, c * D + hi)
                     nc.tensor.matmul_mx(
                         out=bank[:, lo:hi],
                         lhsT=w_codes[step][:, part].bitcast(FP8X4),
                         lhsT_scale=w_scales[step][:, part],
-                        rhs=x_codes[b, c][:, lo:hi].bitcast(FP8X4),
-                        rhs_scale=x_scales[b, c][:, lo:hi],
+                        rhs=x_codes[b][:, columns].bitcast(FP8X4),
+                        rhs_scale=x_scales[b][:, columns],
                         start=(c == 0),
                         stop=(c == PASSES - 1),
                     )
@@ -145,22 +145,24 @@ def tile_token_mixing_swiglu_g2_kernel(tc, x, w_gate, b_gate, w_up, b_up, out_0,
 
         def gate(step, b):
             bank = project(step, b, 0)
-            silu_of[step, b] = work.tile([P, D], F32, name="silu", tag="silu", bufs=4)
+            silu_of[step, b] = work.tile([P, D], F32, name="silu", tag="silu", bufs=8)
             nc.scalar.activation(out=silu_of[step, b][:], in_=bank[:, :D], func=SILU, bias=bias(0, step))
 
         def up(step, b):
             up_of[step, b] = project(step, b, 1)
 
-        def gate_and_up(step, b):
-            gate(step, b)
-            up(step, b)
+        def project_pair(pair):
+            for step, b in pair:
+                gate(step, b)
+            for step, b in pair:
+                up(step, b)
 
         def product(step, b):
             g, t = divmod(step, PACK)
             if g not in y:
-                y[g] = work.tile([P, PACK, M], F32, name="y", tag="y", bufs=3)
+                y[g] = work.tile([P, B, Y_PITCH], F32, name="y", tag="y", bufs=3)
             nc.vector.scalar_tensor_tensor(
-                out=y[g][:, t, b * D : (b + 1) * D],
+                out=y[g][:, b, t * D : (t + 1) * D],
                 in0=up_of[step, b][:, :D],
                 scalar=bias(1, step),
                 in1=silu_of[step, b][:],
@@ -168,37 +170,46 @@ def tile_token_mixing_swiglu_g2_kernel(tc, x, w_gate, b_gate, w_up, b_up, out_0,
                 op1=MULT,
             )
 
-        def store_y(step, b0, b1):
-            g, t = divmod(step, PACK)
-            rows = out_0[b0:b1, g * K_PASS : (g + 1) * K_PASS, :].rearrange("b (p t) d -> p t b d", t=PACK)
-            nc.sync.dma_start(out=rows[:, t], in_=y[g][:, t, b0 * D : b1 * D].rearrange("p (b d) -> p b d", d=D))
-
-        def store_first_y(b):
-            rows = out_0[b, :K_PASS, :].rearrange("(p t) d -> p t d", t=PACK)
-            nc.sync.dma_start(out=rows, in_=y[0][:, :, b * D : (b + 1) * D])
-
-        def open_window(g, lo, hi, wide):
-            if wide:
-                y_side[g, lo] = side_tile("paced")
-            else:
-                y_side[g, lo] = work.tile([P, 256, PACK], BF16, name="y_side", tag="y_side", bufs=6, align_bytes=64)
+        def store_y(g, b0, b1, t0, t1):
+            rows = out_0[b0:b1, g * K_PASS : (g + 1) * K_PASS, :].rearrange("b (p t) d -> p b (t d)", t=PACK)
+            nc.sync.dma_start(out=rows[:, :, t0 * D : t1 * D], in_=y[g][:, b0:b1, t0 * D : t1 * D])
 
         def cast_y(g, start, lo, hi, engine):
-            interleave(engine, y_side[g, start][:, lo - start : hi - start], y[g][:, :, lo:hi])
+            if (g, start) not in y_side:
+                y_side[g, start] = paced_tile() if engine == "gpsimd" else wide_tile()
+            side = y_side[g, start]
+            if engine == "gpsimd" and lo < D < hi:
+                both = y[g][:].rearrange("p b r -> p (b r)")[:, lo : lo + 2 * PACK * D]
+                nc.gpsimd.tensor_scalar(
+                    out=side[:].rearrange("p (h m) t -> p h m t", h=2),
+                    in0=both.rearrange("p (h t d) -> p h d t", h=2, t=PACK)[:, :, : D - lo],
+                    scalar1=1.0,
+                    scalar2=-0.0,
+                    op0=MULT,
+                    op1=ADD,
+                )
+                return
+            for b in range(B):
+                first, end = max(lo, b * D), min(hi, (b + 1) * D)
+                if first < end:
+                    rows = y[g][:, b, : PACK * D].rearrange("p (t d) -> p t d", t=PACK)
+                    interleave(engine, side[:, first - start : end - start], rows[:, :, first - b * D : end - b * D])
 
-        def quantize_y(g, lo, hi, start=None):
-            start = lo if start is None else start
+        def quantize_y(g, start, lo, hi):
             if g not in y_codes:
-                y_codes[g] = work.tile([P, M], U32, name="y_codes", tag="y_codes", bufs=2, align_bytes=64)
-            nc.vector.quantize_mx(
-                out=y_codes[g][:, lo:hi].bitcast(FP8X4),
-                scales=y_scales[PACK * g :, lo:hi],
-                in_=y_side[g, start][:, lo - start : hi - start].rearrange("p m t -> p (m t)"),
-            )
+                y_codes[g] = keep.tile([P, M], U32, name="y_codes%d" % g, align_bytes=64)
+            quantize(y_codes[g][:, lo:hi], y_scales[PACK * g :, lo:hi], y_side[g, start][:, lo - start : hi - start])
 
         def store_codes(g, lo, hi):
             words = out_1[g].rearrange("p m t -> p (m t)").bitcast(I32)
             nc.sync.dma_start(out=words[:, lo:hi], in_=y_codes[g][:, lo:hi].bitcast(I32))
+
+        def store_scales(lo, hi):
+            for q in range(4):
+                (nc.scalar if q % 2 else nc.sync).dma_start(
+                    out=out_2[:, PACK * q : PACK * (q + 1), lo:hi].bitcast(I32),
+                    in_=y_scales[32 * q : 32 * q + PACK * GROUPS, lo:hi].bitcast(I32),
+                )
 
         for kind, i, j in (("x", 0, 0), ("w", 0, 0), ("x", 0, 1), ("w", 0, 1), ("w", 0, 2), ("w", 0, 3)):
             if kind == "x":
@@ -220,128 +231,175 @@ def tile_token_mixing_swiglu_g2_kernel(tc, x, w_gate, b_gate, w_up, b_up, out_0,
         nc.vector.memset(warm[:], 0.0)
         nc.scalar.activation(out=warmed[:], in_=warm[:], func=SILU)
 
-        def x_tile():
-            return work.tile([P, D, PACK], BF16, name="x_side", tag="x_side", bufs=2, align_bytes=64)
-
         def head_x(c):
-            x_side[0, c] = x_tile()
-            copy_x(0, c, 0, HEAD_X[c], "vector")
-            copy_x(0, c, HEAD_X[c], D, "scalar")
-            quantize_x(0, c, N_SPLIT[::-1])
+            side = wide_tile()
+            cut = HEAD_X[c]
+            interleave("vector", side[:, :cut], x_raw[0, c][:, :, :cut])
+            interleave("scalar", side[:, cut:D], x_raw[0, c][:, :, cut:])
+            for lo, hi in N_SPLIT[::-1]:
+                quantize_x(0, c * D + lo, c * D + hi, side[:, lo:hi])
 
-        def head_w(part, on_vector):
+        def head_w(part):
             for t in range(PACK):
-                copy_first_w(t, part, "vector" if t < on_vector else "scalar")
+                copy_first_w(t, part, "vector" if t < HEAD_W[part] else "scalar")
 
+        def copy_x_wide(b, lo, hi, engine):
+            for c, start in enumerate((0, D)):
+                first, end = max(lo, start), min(hi, start + D)
+                if first < end:
+                    interleave(engine, x_wide[b][:, first:end], x_raw[b, c][:, :, first - start : end - start])
+
+        def copy_x_paced(b, engine):
+            x_paced[b] = paced_tile()
+            interleave(engine, x_paced[b][:], x_raw[b, 1][:, :, WIDE - D :])
+
+        def quantize_x_both(b):
+            quantize_x(b, WIDE, X_COLUMNS, x_paced[b][:])
+            quantize_x(b, 0, WIDE, x_wide[b][:])
+
+        slots = [[(t, b) for t in range(PACK)] for b in range(B)]
+        for first in range(PACK, STEPS, PACK):
+            slots.append([(first + t, b) for t in (0, 1) for b in (0, 1)])
+            slots.append([(first + t, b) for t in (2, 3) for b in (0, 1)])
+            slots.append([(first + t, 2) for t in range(PACK)])
+
+        x_wide, x_paced = {}, {}
         for t in range(PACK):
-            w_side[t] = side_tile("paced" if t == PACK - 1 else "free")
+            w_side[t] = wide_tile()
         head_x(0)
-        head_w(0, HEAD_W[0])
+        head_w(0)
         head_x(1)
-        head_w(1, HEAD_W[1])
+        head_w(1)
         quantize_w(0, 0, 256)
         quantize_w(1, 0, 256)
-        head_w(2, HEAD_W[2])
+        head_w(2)
         quantize_w(2, 0, 256)
         quantize_w(3, 0, 256)
-        head_w(3, HEAD_W[3])
+        head_w(3)
+        for step, b in slots[0][:2]:
+            gate(step, b)
+        copy_x_paced(1, "scalar")
+        for step, b in slots[0][2:]:
+            gate(step, b)
         for t in range(PACK):
-            gate(t, 0)
-        for t in range(PACK):
-            quantize_w(t, 256, 512)
-        for t in range(PACK):
-            up(t, 0)
+            quantize_w(t, 256, W_COLUMNS)
+        for step, b in slots[0]:
+            up(step, b)
+        x_wide[1] = wide_tile()
+        copy_x_wide(1, 0, WIDE, "vector")
+        quantize_x_both(1)
 
-        units = [(t, b) for b in range(B) for t in range(PACK)]
-        units += [(step, b) for step in range(PACK, STEPS - 2) for b in range(B)]
-        units += [(STEPS - 2, 0), (STEPS - 2, 1), (STEPS - 1, 0), (STEPS - 1, 1), (STEPS - 2, 2), (STEPS - 1, 2)]
-        sizes = [2, 3, 4] + [B] * (STEPS - 3)
-        paced = {slot: (0, 192 * (slot - 2), 192 * (slot - 1)) for slot in range(2, 8)}
-        paced.update({slot: (1, 256 * (slot - 8), 256 * (slot - 7)) for slot in range(8, 12)})
-        paced.update({slot: (2, 256 * (slot - 12), 256 * (slot - 11)) for slot in range(12, 15)})
-        last = STEPS - 1
-        for slot in range(last):
-            ahead = slot + COPY_LEAD
-            for step, b in units[sum(sizes[:slot]) : sum(sizes[: slot + 1])]:
-                if step >= PACK or b > 0:
-                    gate_and_up(step, b)
+        def products(slot):
+            for step, b in slots[slot]:
                 product(step, b)
-                if step == PACK - 1:
-                    store_first_y(b)
-                if step >= STEPS - 2:
-                    store_y(step, b, b + 1)
-            if PACK <= slot < STEPS - 2:
-                store_y(slot, 0, B)
-            if slot < 2:
-                b = slot + 1
-                on_pool = X_POOL[slot]
-                x_side[b, 0] = side_tile("paced")
-                x_side[b, 1] = x_tile()
-                copy_x(b, 0, 0, on_pool, "gpsimd")
-                copy_x(b, 0, on_pool, D, "scalar")
-                copy_x(b, 1, X_VECTOR[slot], D, "scalar")
-                copy_x(b, 1, 0, X_VECTOR[slot], "vector")
-                quantize_x(b, 0, N_SPLIT[1:])
-                quantize_x(b, 1, N_SPLIT)
-                quantize_x(b, 0, N_SPLIT[:1])
-                continue
-            g, lo, hi = paced[slot]
-            open_window(g, lo, hi, True)
-            cast_y(g, lo, lo, lo + ON_POOL, "gpsimd")
-            cast_y(g, lo, lo + ON_POOL, hi, "scalar")
-            extra = {12: 1, 14: 2}.get(slot)
-            if extra:
-                open_window(extra, 1024, M, False)
-                cast_y(extra, 1024, 1024, M, "scalar")
-            if ahead < STEPS:
-                on_scalar = S_COLUMNS[slot >= 8] - (hi - lo - ON_POOL) - (EXTRA if extra else 0)
-                w_side[ahead] = side_tile("free")
-                copy_w(ahead, 0, on_scalar, "scalar")
-                if on_scalar < 256:
-                    copy_w(ahead, on_scalar, 256, "vector")
-                copy_w(ahead, 256, PARTS * P, "vector")
-                quantize_w(ahead, 0, 256)
-                if extra:
-                    quantize_y(extra, 1024, M)
-                    store_codes(extra, 0, M)
-                if hi - lo == 192:
-                    quantize_y(g, lo + 128, hi, lo)
-                    quantize_y(g, lo, lo + 128)
-                else:
-                    quantize_y(g, lo, hi)
-                quantize_w(ahead, 256, PARTS * P)
+            g, kind = divmod(slot, B)
+            if g == 0 or kind == 2:
+                store_y(g, kind, kind + 1, 0, PACK)
             else:
-                open_window(2, 768, 1024, False)
-                cast_y(2, 768, 768, 1024, "vector")
-                quantize_y(g, lo, hi)
-                quantize_y(2, 768, 1024)
-            if (g, hi) == (0, M):
-                store_codes(0, 0, M)
+                store_y(g, 0, 2, 2 * kind, 2 * kind + 2)
+
+        products(0)
+        copy_x_paced(2, "gpsimd")
+        x_wide[2] = wide_tile()
+        copy_x_wide(2, X_VECTOR, WIDE, "scalar")
+        project_pair(slots[1][:2])
+        project_pair(slots[1][2:])
+        copy_x_wide(2, 0, X_VECTOR, "vector")
+        quantize_x_both(2)
+
+        def pool_window(slot):
+            g, i = divmod(slot - 1, PACK)
+            return g, PACED * i, PACED * i, PACED * (i + 1)
+
+        half = W_COLUMNS // 2
+        for slot in (1, 2):
+            first = PACK + 2 * (slot - 1)
+            cut = W_SCALAR_EARLY[slot - 1]
+            products(slot)
+            cast_y(*pool_window(slot), "gpsimd")
+            if slot == 2:
+                quantize_w(first - 1)
+            project_pair(slots[slot + 1][:2])
+            copy_w(first, 0, half, "scalar")
+            project_pair(slots[slot + 1][2:])
+            copy_w(first + 1, 0, cut, "scalar")
+            copy_w(first, half, W_COLUMNS, "vector")
+            quantize_w(first, 0, half)
+            quantize_w(first, half, W_COLUMNS)
+            quantize_y(*pool_window(slot))
+            copy_w(first + 1, cut, W_COLUMNS, "vector")
+
+        rest = PACK * PACED
+        for slot in range(3, 11):
+            g, kind = divmod(slot, B)
+            ahead = PACK * (g + 1)
+            products(slot)
+            cast_y(*pool_window(slot), "gpsimd")
+            if slot < 9:
+                if kind == 0:
+                    on_scalar = [(ahead + 1, 0, W_CUT // 2), (ahead + 1, W_CUT // 2, W_CUT)]
+                    if slot == 3:
+                        on_scalar = [(ahead, 0, W_SCALAR), (ahead + 1, 0, W_CUT)]
+                    on_vector, ready = ahead, [ahead - 1]
+                elif kind == 1:
+                    on_scalar = [(ahead + 1, W_CUT, W_COLUMNS), (ahead + 2, 0, W_SCALAR)]
+                    on_vector, ready = ahead + 2, [ahead]
+                else:
+                    on_scalar = [(ahead + 3, 0, W_SCALAR), (ahead + PACK, 0, W_SCALAR)]
+                    on_vector, ready = ahead + 3, [ahead + 1, ahead + 2]
+                for step in ready:
+                    quantize_w(step)
+                project_pair(slots[slot + 1][:2])
+                if slot == 8:
+                    cast_y(0, rest, rest, M, "scalar")
+                    on_scalar.reverse()
+                else:
+                    copy_w(*on_scalar[0], "scalar")
+                project_pair(slots[slot + 1][2:])
+                copy_w(*on_scalar[1], "scalar")
+                quantize_y(*pool_window(slot))
+                copy_w(on_vector, W_SCALAR, W_COLUMNS, "vector")
+                if slot in (4, 8):
+                    store_codes(slot // PACK - 1, 0, rest)
+            elif slot == 9:
+                quantize_w(STEPS - 1)
+                quantize_y(0, rest, rest, M)
+                store_codes(0, rest, M)
+                project_pair(slots[slot + 1][:2])
+                cast_y(1, rest, rest, M, "scalar")
+                project_pair(slots[slot + 1][2:])
+                cast_y(2, WIDE, WIDE, WIDE + Y_SCALAR[0], "scalar")
+                quantize_y(*pool_window(slot))
+                cast_y(2, WIDE, WIDE + Y_SCALAR[0], rest, "vector")
+            else:
+                quantize_y(1, rest, rest, M)
+                store_codes(1, rest, M)
+                project_pair(slots[slot + 1][:2])
+                cast_y(2, rest, rest, M, "scalar")
+                project_pair(slots[slot + 1][2:])
+                cast_y(3, 0, WIDE - Y_SCALAR[1], WIDE, "scalar")
+                quantize_y(2, WIDE, WIDE, rest)
+                quantize_y(*pool_window(slot))
+                store_codes(2, 0, rest)
+                cast_y(3, 0, 0, WIDE - Y_SCALAR[1], "vector")
 
         g = GROUPS - 1
-        for step, b in units[-B:]:
-            gate_and_up(step, b)
+        cast_y(g, WIDE, WIDE, 2 * D, "gpsimd")
+        for step, b in slots[-1][:2]:
             product(step, b)
-            store_y(step, b, b + 1)
-        for lo, hi, engine in ((0, 128, "gpsimd"), (128, 384, "scalar"), (384, 640, "scalar"), (640, 768, "vector")):
-            open_window(g, lo, hi, engine == "gpsimd")
-            cast_y(g, lo, lo, hi, engine)
-        quantize_y(2, 1024, M)
-        store_codes(2, 0, M)
-        quantize_y(g, 0, 128)
-        quantize_y(g, 128, 384)
-        store_codes(g, 0, 384)
-        for lo, hi, engine in ((768, 1024, "vector"), (1024, M, "scalar")):
-            open_window(g, lo, hi, False)
-            cast_y(g, lo, lo, hi, engine)
-        quantize_y(g, 640, 768)
-        quantize_y(g, 384, 640)
-        store_codes(g, 384, 768)
-        quantize_y(g, 768, 1024)
-        quantize_y(g, 1024, M)
-        store_codes(g, 768, M)
-        for q in range(4):
-            (nc.scalar if q % 2 else nc.sync).dma_start(
-                out=out_2[:, PACK * q : PACK * (q + 1), :].bitcast(I32),
-                in_=y_scales[32 * q : 32 * q + PACK * GROUPS, :].bitcast(I32),
-            )
+        store_y(g, B - 1, B, 0, 2)
+        for step, b in slots[-1][2:]:
+            product(step, b)
+        store_y(g, B - 1, B, 2, PACK)
+        cut = 2 * D + P
+        cast_y(g, cut, cut, M, "scalar")
+        quantize_y(g, 0, 0, WIDE)
+        store_codes(g, 0, WIDE)
+        quantize_y(g - 1, rest, rest, M)
+        store_codes(g - 1, rest, M)
+        cast_y(g, 2 * D, 2 * D, cut, "vector")
+        quantize_y(g, WIDE, WIDE, 2 * D)
+        quantize_y(g, 2 * D, 2 * D, cut)
+        quantize_y(g, cut, cut, M)
+        store_codes(g, WIDE, M)
+        store_scales(0, M)

from contextlib import ExitStack

import concourse.mybir as mybir

B, S, D, F = 3, 1024, 384, 2048
FLOPS = 2 * 2 * F * S * B * D

F32 = mybir.dt.float32
BF16 = mybir.dt.bfloat16
I32 = mybir.dt.int32
U32 = mybir.dt.uint32
U8 = mybir.dt.uint8
FP8X4 = mybir.dt.float8_e4m3fn_x4
SILU = mybir.ActivationFunctionType.Silu
ADD = mybir.AluOpType.add
MULT = mybir.AluOpType.mult

P = 128
PACK = 4
K_PASS = P * PACK
PASSES = S // K_PASS
GROUPS = F // K_PASS
M = B * D
STEPS = GROUPS * PACK
PARTS = 2 * PASSES
W_COLUMNS = PARTS * P
X_COLUMNS = PASSES * D
N_SPLIT = ((0, 256), (256, D))
WIDE = 512
PACED = 256
HEAD_W = (3, 2, 3, 2)
HEAD_X = (256, 256)
X_VECTOR = 224
W_SCALAR = 192
W_SCALAR_EARLY = (256, 320)
W_CUT = 336
Y_SCALAR = (256, 256)
W_RUN = 4
Y_PITCH = PACK * D + PACED


def tile_token_mixing_swiglu_g2_kernel(tc, x, w_gate, b_gate, w_up, b_up, out_0, out_1, out_2):
    nc = tc.nc
    weights = (w_gate, w_up)

    with ExitStack() as ctx:
        keep = ctx.enter_context(tc.tile_pool(name="keep", bufs=1))
        work = ctx.enter_context(tc.tile_pool(name="work", bufs=1))
        psum = ctx.enter_context(tc.psum_pool(name="psum", bufs=4))
        ctx.enter_context(tc.manual_schedule())

        x_raw, x_codes, x_scales = {}, {}, {}
        w_raw, w_side, w_codes, w_scales = {}, {}, {}, {}
        y, y_side, y_codes, silu_of, up_of = {}, {}, {}, {}, {}
        bias_first = [keep.tile([P, 1, PACK], BF16, name="bias_first%d" % i) for i in range(2)]
        bias_rest = [keep.tile([P, GROUPS - 1, PACK], BF16, name="bias_rest%d" % i) for i in range(2)]
        y_scales = keep.tile([P, M], U8, name="y_scales", align_bytes=64)

        def bias(which, step):
            g, t = divmod(step, PACK)
            return bias_first[which][:, 0, t : t + 1] if g == 0 else bias_rest[which][:, g - 1, t : t + 1]

        def interleave(engine, dst, src, run=4):
            if engine == "gpsimd":
                nc.gpsimd.tensor_scalar(
                    out=dst, in0=src.rearrange("p j m -> p m j"), scalar1=1.0, scalar2=-0.0, op0=MULT, op1=ADD
                )
                return
            out = dst.rearrange("p (n i) j -> p n j i", i=run)
            in_ = src.rearrange("p j (n i) -> p n j i", i=run)
            if engine == "vector":
                nc.vector.tensor_copy(out=out, in_=in_)
            else:
                nc.scalar.copy(out=out, in_=in_)

        def quantize(codes, scales, side):
            nc.vector.quantize_mx(out=codes.bitcast(FP8X4), scales=scales, in_=side.rearrange("p m j -> p (m j)"))

        def wide_tile():
            return work.tile([P, WIDE, PACK], BF16, name="wide", tag="wide", bufs=6, align_bytes=64)

        def paced_tile():
            return work.tile([P, PACED, PACK], BF16, name="paced", tag="paced", bufs=1, align_bytes=64)

        def load_x(b, c):
            x_raw[b, c] = keep.tile([P, PACK, D], BF16, name="x_raw%d_%d" % (b, c))
            rows = x[b, c * K_PASS : (c + 1) * K_PASS, :]
            nc.sync.dma_start(out=x_raw[b, c][:], in_=rows.rearrange("(p j) d -> p j d", j=PACK))

        def load_w(g, part):
            c = part % PASSES
            if g == 0:
                w_raw[g, part] = keep.tile([P, PACK, K_PASS], BF16, name="w_first%d" % part)
                dst = w_raw[g, part][:]
            else:
                if g not in w_raw:
                    w_raw[g] = keep.tile([P, PACK, PARTS, K_PASS], BF16, name="w_raw%d" % g)
                dst = w_raw[g][:, :, part]
            rows = weights[part // PASSES][c * K_PASS : (c + 1) * K_PASS, g * K_PASS : (g + 1) * K_PASS]
            nc.sync.dma_start(out=dst, in_=rows.rearrange("(p j) f -> p j f", j=PACK))

        def load_bias(tiles, g0, g1):
            for tile, vec in zip(tiles, (b_gate, b_up)):
                nc.sync.dma_start(out=tile[:], in_=vec.rearrange("(g p t) -> p g t", p=P, t=PACK)[:, g0:g1])

        def quantize_x(b, lo, hi, side):
            if b not in x_codes:
                x_codes[b] = keep.tile([P, X_COLUMNS], U32, name="x_codes%d" % b, align_bytes=64)
                x_scales[b] = keep.tile([P, X_COLUMNS], U8, name="x_scales%d" % b, align_bytes=64)
            quantize(x_codes[b][:, lo:hi], x_scales[b][:, lo:hi], side)

        def copy_first_w(t, part, engine):
            src = w_raw[0, part][:].rearrange("p j (m t) -> p t j m", t=PACK)[:, t]
            interleave(engine, w_side[t][:, part * P : (part + 1) * P], src, W_RUN)

        def copy_w(step, lo, hi, engine):
            g, t = divmod(step, PACK)
            if step not in w_side:
                w_side[step] = wide_tile()
            src = w_raw[g][:].rearrange("p j a (m t) -> p t j (a m)", t=PACK)[:, t]
            interleave(engine, w_side[step][:, lo:hi], src[:, :, lo:hi], W_RUN)

        def quantize_w(step, lo=0, hi=W_COLUMNS):
            if step not in w_codes:
                w_codes[step] = work.tile([P, W_COLUMNS], U32, name="w_codes", tag="w_codes", bufs=7, align_bytes=64)
                w_scales[step] = work.tile([P, W_COLUMNS], U8, name="w_scales", tag="w_scales", bufs=7, align_bytes=64)
            quantize(w_codes[step][:, lo:hi], w_scales[step][:, lo:hi], w_side[step][:, lo:hi])

        def project(step, b, which):
            bank = psum.tile([P, 512], F32, name="bank%d" % which, tag="bank%d" % which)
            for lo, hi in N_SPLIT:
                for c in range(PASSES):
                    part = slice((which * PASSES + c) * P, (which * PASSES + c + 1) * P)
                    columns = slice(c * D + lo, c * D + hi)
                    nc.tensor.matmul_mx(
                        out=bank[:, lo:hi],
                        lhsT=w_codes[step][:, part].bitcast(FP8X4),
                        lhsT_scale=w_scales[step][:, part],
                        rhs=x_codes[b][:, columns].bitcast(FP8X4),
                        rhs_scale=x_scales[b][:, columns],
                        start=(c == 0),
                        stop=(c == PASSES - 1),
                    )
            return bank

        def gate(step, b):
            bank = project(step, b, 0)
            silu_of[step, b] = work.tile([P, D], F32, name="silu", tag="silu", bufs=8)
            nc.scalar.activation(out=silu_of[step, b][:], in_=bank[:, :D], func=SILU, bias=bias(0, step))

        def up(step, b):
            up_of[step, b] = project(step, b, 1)

        def project_pair(pair):
            for step, b in pair:
                gate(step, b)
            for step, b in pair:
                up(step, b)

        def product(step, b):
            g, t = divmod(step, PACK)
            if g not in y:
                y[g] = work.tile([P, B, Y_PITCH], F32, name="y", tag="y", bufs=3)
            nc.vector.scalar_tensor_tensor(
                out=y[g][:, b, t * D : (t + 1) * D],
                in0=up_of[step, b][:, :D],
                scalar=bias(1, step),
                in1=silu_of[step, b][:],
                op0=ADD,
                op1=MULT,
            )

        def store_y(g, b0, b1, t0, t1):
            rows = out_0[b0:b1, g * K_PASS : (g + 1) * K_PASS, :].rearrange("b (p t) d -> p b (t d)", t=PACK)
            nc.sync.dma_start(out=rows[:, :, t0 * D : t1 * D], in_=y[g][:, b0:b1, t0 * D : t1 * D])

        def cast_y(g, start, lo, hi, engine):
            if (g, start) not in y_side:
                y_side[g, start] = paced_tile() if engine == "gpsimd" else wide_tile()
            side = y_side[g, start]
            if engine == "gpsimd" and lo < D < hi:
                both = y[g][:].rearrange("p b r -> p (b r)")[:, lo : lo + 2 * PACK * D]
                nc.gpsimd.tensor_scalar(
                    out=side[:].rearrange("p (h m) t -> p h m t", h=2),
                    in0=both.rearrange("p (h t d) -> p h d t", h=2, t=PACK)[:, :, : D - lo],
                    scalar1=1.0,
                    scalar2=-0.0,
                    op0=MULT,
                    op1=ADD,
                )
                return
            for b in range(B):
                first, end = max(lo, b * D), min(hi, (b + 1) * D)
                if first < end:
                    rows = y[g][:, b, : PACK * D].rearrange("p (t d) -> p t d", t=PACK)
                    interleave(engine, side[:, first - start : end - start], rows[:, :, first - b * D : end - b * D])

        def quantize_y(g, start, lo, hi):
            if g not in y_codes:
                y_codes[g] = keep.tile([P, M], U32, name="y_codes%d" % g, align_bytes=64)
            quantize(y_codes[g][:, lo:hi], y_scales[PACK * g :, lo:hi], y_side[g, start][:, lo - start : hi - start])

        def store_codes(g, lo, hi):
            words = out_1[g].rearrange("p m t -> p (m t)").bitcast(I32)
            nc.sync.dma_start(out=words[:, lo:hi], in_=y_codes[g][:, lo:hi].bitcast(I32))

        def store_scales(lo, hi):
            for q in range(4):
                (nc.scalar if q % 2 else nc.sync).dma_start(
                    out=out_2[:, PACK * q : PACK * (q + 1), lo:hi].bitcast(I32),
                    in_=y_scales[32 * q : 32 * q + PACK * GROUPS, lo:hi].bitcast(I32),
                )

        for kind, i, j in (("x", 0, 0), ("w", 0, 0), ("x", 0, 1), ("w", 0, 1), ("w", 0, 2), ("w", 0, 3)):
            if kind == "x":
                load_x(i, j)
            else:
                load_w(i, j)
        load_bias(bias_first, 0, 1)
        for b in range(1, B):
            for c in range(PASSES):
                load_x(b, c)
        for g in range(1, GROUPS):
            for part in range(PARTS):
                load_w(g, part)
            if g == 1:
                load_bias(bias_rest, 1, GROUPS)

        warm = keep.tile([P, 8], F32)
        warmed = keep.tile([P, 8], F32)
        nc.vector.memset(warm[:], 0.0)
        nc.scalar.activation(out=warmed[:], in_=warm[:], func=SILU)

        def head_x(c):
            side = wide_tile()
            cut = HEAD_X[c]
            interleave("vector", side[:, :cut], x_raw[0, c][:, :, :cut])
            interleave("scalar", side[:, cut:D], x_raw[0, c][:, :, cut:])
            for lo, hi in N_SPLIT[::-1]:
                quantize_x(0, c * D + lo, c * D + hi, side[:, lo:hi])

        def head_w(part):
            for t in range(PACK):
                copy_first_w(t, part, "vector" if t < HEAD_W[part] else "scalar")

        def copy_x_wide(b, lo, hi, engine):
            for c, start in enumerate((0, D)):
                first, end = max(lo, start), min(hi, start + D)
                if first < end:
                    interleave(engine, x_wide[b][:, first:end], x_raw[b, c][:, :, first - start : end - start])

        def copy_x_paced(b, engine):
            x_paced[b] = paced_tile()
            interleave(engine, x_paced[b][:], x_raw[b, 1][:, :, WIDE - D :])

        def quantize_x_both(b):
            quantize_x(b, WIDE, X_COLUMNS, x_paced[b][:])
            quantize_x(b, 0, WIDE, x_wide[b][:])

        slots = [[(t, b) for t in range(PACK)] for b in range(B)]
        for first in range(PACK, STEPS, PACK):
            slots.append([(first + t, b) for t in (0, 1) for b in (0, 1)])
            slots.append([(first + t, b) for t in (2, 3) for b in (0, 1)])
            slots.append([(first + t, 2) for t in range(PACK)])

        x_wide, x_paced = {}, {}
        for t in range(PACK):
            w_side[t] = wide_tile()
        head_x(0)
        head_w(0)
        head_x(1)
        head_w(1)
        quantize_w(0, 0, 256)
        quantize_w(1, 0, 256)
        head_w(2)
        quantize_w(2, 0, 256)
        quantize_w(3, 0, 256)
        head_w(3)
        for step, b in slots[0][:2]:
            gate(step, b)
        copy_x_paced(1, "scalar")
        for step, b in slots[0][2:]:
            gate(step, b)
        for t in range(PACK):
            quantize_w(t, 256, W_COLUMNS)
        for step, b in slots[0]:
            up(step, b)
        x_wide[1] = wide_tile()
        copy_x_wide(1, 0, WIDE, "vector")
        quantize_x_both(1)

        def products(slot):
            for step, b in slots[slot]:
                product(step, b)
            g, kind = divmod(slot, B)
            if g == 0 or kind == 2:
                store_y(g, kind, kind + 1, 0, PACK)
            else:
                store_y(g, 0, 2, 2 * kind, 2 * kind + 2)

        products(0)
        copy_x_paced(2, "gpsimd")
        x_wide[2] = wide_tile()
        copy_x_wide(2, X_VECTOR, WIDE, "scalar")
        project_pair(slots[1][:2])
        project_pair(slots[1][2:])
        copy_x_wide(2, 0, X_VECTOR, "vector")
        quantize_x_both(2)

        def pool_window(slot):
            g, i = divmod(slot - 1, PACK)
            return g, PACED * i, PACED * i, PACED * (i + 1)

        half = W_COLUMNS // 2
        for slot in (1, 2):
            first = PACK + 2 * (slot - 1)
            cut = W_SCALAR_EARLY[slot - 1]
            products(slot)
            cast_y(*pool_window(slot), "gpsimd")
            if slot == 2:
                quantize_w(first - 1)
            project_pair(slots[slot + 1][:2])
            copy_w(first, 0, half, "scalar")
            project_pair(slots[slot + 1][2:])
            copy_w(first + 1, 0, cut, "scalar")
            copy_w(first, half, W_COLUMNS, "vector")
            quantize_w(first, 0, half)
            quantize_w(first, half, W_COLUMNS)
            quantize_y(*pool_window(slot))
            copy_w(first + 1, cut, W_COLUMNS, "vector")

        rest = PACK * PACED
        for slot in range(3, 11):
            g, kind = divmod(slot, B)
            ahead = PACK * (g + 1)
            products(slot)
            cast_y(*pool_window(slot), "gpsimd")
            if slot < 9:
                if kind == 0:
                    on_scalar = [(ahead + 1, 0, W_CUT // 2), (ahead + 1, W_CUT // 2, W_CUT)]
                    if slot == 3:
                        on_scalar = [(ahead, 0, W_SCALAR), (ahead + 1, 0, W_CUT)]
                    on_vector, ready = ahead, [ahead - 1]
                elif kind == 1:
                    on_scalar = [(ahead + 1, W_CUT, W_COLUMNS), (ahead + 2, 0, W_SCALAR)]
                    on_vector, ready = ahead + 2, [ahead]
                else:
                    on_scalar = [(ahead + 3, 0, W_SCALAR), (ahead + PACK, 0, W_SCALAR)]
                    on_vector, ready = ahead + 3, [ahead + 1, ahead + 2]
                for step in ready:
                    quantize_w(step)
                project_pair(slots[slot + 1][:2])
                if slot == 8:
                    cast_y(0, rest, rest, M, "scalar")
                    on_scalar.reverse()
                else:
                    copy_w(*on_scalar[0], "scalar")
                project_pair(slots[slot + 1][2:])
                copy_w(*on_scalar[1], "scalar")
                quantize_y(*pool_window(slot))
                copy_w(on_vector, W_SCALAR, W_COLUMNS, "vector")
                if slot in (4, 8):
                    store_codes(slot // PACK - 1, 0, rest)
            elif slot == 9:
                quantize_w(STEPS - 1)
                quantize_y(0, rest, rest, M)
                store_codes(0, rest, M)
                project_pair(slots[slot + 1][:2])
                cast_y(1, rest, rest, M, "scalar")
                project_pair(slots[slot + 1][2:])
                cast_y(2, WIDE, WIDE, WIDE + Y_SCALAR[0], "scalar")
                quantize_y(*pool_window(slot))
                cast_y(2, WIDE, WIDE + Y_SCALAR[0], rest, "vector")
            else:
                quantize_y(1, rest, rest, M)
                store_codes(1, rest, M)
                project_pair(slots[slot + 1][:2])
                cast_y(2, rest, rest, M, "scalar")
                project_pair(slots[slot + 1][2:])
                cast_y(3, 0, WIDE - Y_SCALAR[1], WIDE, "scalar")
                quantize_y(2, WIDE, WIDE, rest)
                quantize_y(*pool_window(slot))
                store_codes(2, 0, rest)
                cast_y(3, 0, 0, WIDE - Y_SCALAR[1], "vector")

        g = GROUPS - 1
        cast_y(g, WIDE, WIDE, 2 * D, "gpsimd")
        for step, b in slots[-1][:2]:
            product(step, b)
        store_y(g, B - 1, B, 0, 2)
        for step, b in slots[-1][2:]:
            product(step, b)
        store_y(g, B - 1, B, 2, PACK)
        cut = 2 * D + P
        cast_y(g, cut, cut, M, "scalar")
        quantize_y(g, 0, 0, WIDE)
        store_codes(g, 0, WIDE)
        quantize_y(g - 1, rest, rest, M)
        store_codes(g - 1, rest, M)
        cast_y(g, 2 * D, 2 * D, cut, "vector")
        quantize_y(g, WIDE, WIDE, 2 * D)
        quantize_y(g, 2 * D, 2 * D, cut)
        quantize_y(g, cut, cut, M)
        store_codes(g, WIDE, M)
        store_scales(0, M)
